import numpy as np
import ml_dtypes


def mxq(x, axis, fmt="e4m3"):
    dtype, down = {"e4m3": (ml_dtypes.float8_e4m3fn, 7), "e5m2": (ml_dtypes.float8_e5m2, 14)}[fmt]
    v = np.moveaxis(np.asarray(x, np.float32).astype(ml_dtypes.bfloat16).astype(np.float64), axis, -1)
    blocks = v.reshape(v.shape[:-1] + (-1, 32))
    amax = np.abs(blocks).max(-1, keepdims=True)
    byte = np.maximum(np.where(amax > 0, np.frexp(amax)[1] - 1 + 127, 0) - down, 1)
    scale = np.exp2(byte - 127.0)
    codes = (blocks / scale).astype(np.float32).astype(dtype).astype(np.float64)
    return np.moveaxis((codes * scale).reshape(v.shape), -1, axis)


WIDE = False


def mx_kscale(k, group=512):
    if not WIDE:
        return np.ones(k)
    levels = np.array([10, -10, 5, -5, 0])
    if group != 512:
        return np.exp2(np.random.permutation(np.resize(levels, k // group))).repeat(group)
    if k % 512:
        return np.exp2(np.random.permutation(np.resize(levels, k // 32))).repeat(32)
    a = np.empty((k // 512, 16))
    for p in range(k // 512):
        a[p, :8] = np.random.permutation(np.resize(levels, 8))
        for g in range(8):
            far = levels[np.abs(levels - a[p, g]) >= 10]
            a[p, g + 8] = far[np.random.randint(len(far))]
    return np.exp2(a.ravel()).repeat(32)


def f64(x):
    return np.asarray(x).astype(np.float64)


def striped(idx):
    return np.tile(np.asarray(idx).reshape(-1, 16).T, (8, 1)).astype(np.uint16)


def unstriped(offs):
    return offs[:16].T.reshape(-1).astype(np.int64)


H, KV, D, NQ, N = 8, 8, 128, 512, 512


def setup_inputs():
    n = np.random.standard_normal
    s = mx_kscale(D, 0)[:, None]
    u = mx_kscale(N)
    t = np.random.uniform(0.5, 2.0, N) * u
    v = n((KV, N, 128))
    return {
        "qT": (n((H, D, NQ)) * s * (0.70 / np.sqrt(D))).astype(np.float32),
        "kT": (n((KV, D, N)) / s).astype(np.float32),
        "t": t.reshape(N, 1).astype(np.float32),
        "v": (v / t[:, None]).astype(np.float32),
        "kb": (0.5 * n((N, 1))).astype(np.float32),
        "og": n((H, NQ, 128)).astype(np.float32),
    }


def reference(qT, kT, t, v, kb, og):
    a = mxq(f64(kT), 1, "e4m3").transpose(0, 2, 1) @ mxq(f64(qT), 1, "e4m3")
    a = a + f64(kb)
    p = 1.0 / (1.0 + np.exp(-a))
    w = p * f64(t)
    y = mxq(w, 1, "e4m3").transpose(0, 2, 1) @ mxq(f64(v), 1, "e4m3")
    y = y / 16.0
    y = y / (1.0 + np.exp(-f64(og)))
    return y

@@ -1,0 +1,235 @@
+from contextlib import ExitStack
+
+import concourse.mybir as mybir
+
+H, D, NQ, N, E = 8, 128, 512, 512, 128
+FLOPS = 2 * H * N * NQ * (D + E)
+
+F32 = mybir.dt.float32
+BF16 = mybir.dt.bfloat16
+U32 = mybir.dt.uint32
+U8 = mybir.dt.uint8
+FP8X4 = mybir.dt.float8_e4m3fn_x4
+SIGMOID = mybir.ActivationFunctionType.Sigmoid
+MULT = mybir.AluOpType.mult
+
+P = 128
+ROWS = 32
+BANKS = (2, 1, 1, 2)
+Y_BANKS = 2
+P_BUFS = 8
+W_BUFS = 8
+
+LOADS = "Lk0a Lk0b Lq0a Lq0b Lk1 Lq1 Lv45 Lv23 Lv67 Lg45 Lg01 Lg67 Lv01 Lg23".split()
+ORDER = """
+S:ck0a ck0b qk023 qk01 qk00 cq0a qq0a cq0b M0a0 M0a1 qq0b A0a1 A0a0 M10 A0a2 A0a3
+M30 A10 ck1a1 M31 ck1a0 A30 T0a M12 A31 M33 A12 ck1b0 M32 ck1b1 A33 M0b0
+cq1a0 cq1b0 A32 M11 cq1b1 cq1a1 A0b1 M0b1 qk1 A11 M20 qq1 A0b2 M13 A0b0 T3
+A0b3 M7a0 A20 M41 A13 M21 A7a0 A41 M42 T0b A21 M52 A42 T1 M22 A52
+M43 A22 M40 A43 M23 W0 A40 M50 W1 A23 M7a1 T4 S:cv1 A50 S:cv5 M51
+S:cv0 M62 T2 S:cv4 A7a1 A7a2 A51 A62 M53 qv01 W4 G0 M61 qv45 A53 M7b0
+W3 A61 P4 T5 S:cv2 P0 G4 M60 A7a3 A7b1 M7b1 A60 W2 S:cv7 F4 M63
+T7a A7b3 A7b0 G6 F0 A63 W7a S:cv3 W5 G2 T6 P5 G5 P1 G7 S:cv6
+G1 F5 A7b2 qv23 G3 qv67 F1 P3 W6 P7a F3 F7a P6 T7b P2 F6
+W7b F2 P7b F7b
+""".split()
+
+
+def tile_rows_a_sigmoid_kb_gate_kernel(tc, qT, kT, t, v, kb, og, out):
+    nc = tc.nc
+    with ExitStack() as ctx:
+        sb = ctx.enter_context(tc.tile_pool(name="sb", bufs=1))
+        ps = ctx.enter_context(tc.psum_pool(name="ps", bufs=1))
+        ctx.enter_context(tc.manual_schedule())
+
+        def tiles(name, count, shape, dtype, pool=sb):
+            if pool is ps:
+                return [pool.tile(shape, dtype, name="%s%d" % (name, i)) for i in range(count)]
+            return [pool.tile(shape, dtype, name="%s%d" % (name, i), align_bytes=64) for i in range(count)]
+
+        t_sb, kb_sb = tiles("col", 2, [P, 4], F32)
+        nc.scalar.dma_start(out=kb_sb[:], in_=kb.rearrange("(p j) o -> p (j o)", j=4))
+        nc.scalar.dma_start(out=t_sb[:], in_=t.rearrange("(p j) o -> p (j o)", j=4))
+
+        raw = {}
+        for name in LOADS:
+            kind = name[1]
+            if kind in "qk":
+                s = int(name[2])
+                src = (qT if kind == "q" else kT)[4 * s : 4 * s + 4].rearrange("g (p j) n -> (g p) j n", j=4)
+                if len(name) == 4:
+                    u = "ab".index(name[3])
+                    tl = sb.tile([P, 4, 256], F32, name=name, align_bytes=64)
+                    nc.sync.dma_start(out=tl[:], in_=src[:, :, 256 * u : 256 * u + 256])
+                    raw[kind, s, u] = tl[:]
+                else:
+                    tl = sb.tile([P, 4, 512], F32, name=name, align_bytes=64)
+                    nc.sync.dma_start(out=tl[:], in_=src)
+                    for u in range(2):
+                        raw[kind, s, u] = tl[:, :, 256 * u : 256 * u + 256]
+            else:
+                h0, cnt = int(name[2]), len(name) - 2
+                tl = sb.tile([P, cnt, 512], F32, name=name, align_bytes=64)
+                if kind == "v":
+                    nc.sync.dma_start(out=tl[:], in_=v[h0 : h0 + cnt].rearrange("h (p j) e -> p h (j e)", j=4))
+                else:
+                    nc.sync.dma_start(
+                        out=tl[:].rearrange("p h (u x) -> p (h u) x", u=2),
+                        in_=og[h0 : h0 + cnt].rearrange("h (u m c) e -> m (h u) (c e)", u=2, c=2),
+                    )
+                for i in range(cnt):
+                    raw[kind, h0 + i] = tl[:, i, :]
+
+        q_bf = tiles("q_bf", 2, [P, 2, 2, 128, 4], BF16)
+        k_bf = tiles("k_bf", 2, [P, 4, 128, 4], BF16)
+        v_bf = tiles("v_bf", 1, [P, H, 128, 4], BF16)[0]
+        q_codes = tiles("q_codes", 2, [P, 512], U32)
+        k_codes = tiles("k_codes", 2, [P, 512], U32)
+        v_codes = tiles("v_codes", 1, [P, H * 128], U32)[0]
+        q_scales = tiles("q_scales", 2, [P, 512], U8)
+        k_scales = tiles("k_scales", 2, [P, 512], U8)
+        v_scales = tiles("v_scales", 1, [P, H * 128], U8)[0]
+        p_sb = tiles("p", P_BUFS, [P, 4, 512], F32)
+        w_bf = tiles("w_bf", W_BUFS, [P, 512, 4], BF16)
+        w_codes = tiles("w_codes", W_BUFS, [P, 512], U32)
+        w_scales = tiles("w_scales", W_BUFS, [P, 512], U8)
+        banks = [tiles("score%d_" % g, BANKS[g], [P, 512], F32, ps) for g in range(4)]
+        y_banks = tiles("y", Y_BANKS, [P, 512], F32, ps)
+        y_of = {}
+        used = [0, 0, 0, 0]
+        where = {}
+
+        def copy(eng, dst, src):
+            if eng == "S":
+                nc.scalar.copy(out=dst, in_=src)
+            elif eng == "G":
+                nc.gpsimd.tensor_scalar(out=dst, in0=src, scalar1=1.0, scalar2=1.0, op0=MULT, op1=MULT)
+            else:
+                nc.vector.tensor_copy(out=dst, in_=src)
+
+        def quantize(codes, scales, src):
+            nc.vector.quantize_mx(out=codes.bitcast(FP8X4), scales=scales, in_=src)
+
+        def span(unit):
+            return (0, 512) if len(unit) == 1 else (256 * "ab".index(unit[1]), 256)
+
+        for item in ORDER:
+            eng, op = item.split(":") if ":" in item else ("V", item)
+            if op[:2] in ("cq", "ck"):
+                s, u = int(op[2]), "ab".index(op[3])
+                lo, n = (0, 256) if len(op) == 4 else (128 * int(op[4]), 128)
+                src = raw[op[1], s, u][:, :, lo : lo + n]
+                if op[1] == "q":
+                    dst = q_bf[s][:, u, :, lo // 2 : (lo + n) // 2, :]
+                    copy(eng, dst.rearrange("p c m j -> p m j c"), src.rearrange("p j (m c) -> p m j c", c=2))
+                else:
+                    s0 = (256 * u + lo) // 4
+                    dst = k_bf[s][:, :, s0 : s0 + n // 4, :]
+                    copy(eng, dst.rearrange("p r s j -> p s j r"), src.rearrange("p j (s r) -> p s j r", r=4))
+            elif op[:2] == "cv":
+                h = int(op[2])
+                copy(
+                    eng,
+                    v_bf[:, h, :, :].rearrange("p (c i) j -> p c j i", i=2),
+                    raw["v", h].rearrange("p (j c i) -> p c j i", j=4, i=2),
+                )
+            elif op[:2] == "qq":
+                s = int(op[2])
+                lo, n = span(op[2:])
+                flat = q_bf[s][:].rearrange("p u c m j -> p (u c m j)")
+                quantize(q_codes[s][:, lo : lo + n], q_scales[s][:, lo : lo + n], flat[:, 4 * lo : 4 * (lo + n)])
+            elif op[:2] == "qk":
+                s = int(op[2])
+                lo, n = (0, 512) if len(op) == 3 else (128 * int(op[3]), 128 * (len(op) - 3))
+                flat = k_bf[s][:].rearrange("p r s j -> p (r s j)")
+                quantize(k_codes[s][:, lo : lo + n], k_scales[s][:, lo : lo + n], flat[:, 4 * lo : 4 * (lo + n)])
+            elif op[:2] == "qv":
+                lo, n = 128 * int(op[2]), 128 * (len(op) - 2)
+                flat = v_bf[:].rearrange("p h e j -> p (h e j)")
+                quantize(v_codes[:, lo : lo + n], v_scales[:, lo : lo + n], flat[:, 4 * lo : 4 * (lo + n)])
+            elif op[0] == "M":
+                unit, i = op[1:-1], int(op[-1])
+                h = int(unit[0])
+                s, g = divmod(h, 4)
+                lo, n = span(unit)
+                bank = banks[g][used[g] % BANKS[g]]
+                used[g] += 1
+                rows = slice(ROWS * g, ROWS * (g + 1))
+                rs = [i] if n == 512 else [2 * i, 2 * i + 1]
+                for x, r in enumerate(rs):
+                    where[unit, r] = bank[:, x * n : (x + 1) * n]
+                    for b in range(n // 128):
+                        qc = slice(lo + 128 * b, lo + 128 * (b + 1))
+                        kc = slice(128 * r, 128 * (r + 1))
+                        nc.tensor.matmul_mx(
+                            out=bank[:, x * n + 128 * b : x * n + 128 * (b + 1)],
+                            lhsT=k_codes[s][rows, kc].bitcast(FP8X4),
+                            lhsT_scale=k_scales[s][rows, kc],
+                            rhs=q_codes[s][rows, qc].bitcast(FP8X4),
+                            rhs_scale=q_scales[s][rows, qc],
+                            start=True,
+                            stop=True,
+                        )
+            elif op[0] == "A":
+                unit, r = op[1:-1], int(op[-1])
+                lo, n = span(unit)
+                nc.scalar.activation(
+                    out=p_sb[int(unit[0]) % P_BUFS][:, r, lo : lo + n],
+                    in_=where[unit, r],
+                    func=SIGMOID,
+                    bias=kb_sb[:, r : r + 1],
+                )
+            elif op[0] == "T":
+                h = int(op[1])
+                lo, n = span(op[1:])
+                nc.vector.tensor_tensor(
+                    out=w_bf[h % W_BUFS][:, lo : lo + n, :].rearrange("p (c i) r -> p c r i", i=2),
+                    in0=p_sb[h % P_BUFS][:, :, lo : lo + n].rearrange("p r (c i) -> p c r i", i=2),
+                    in1=t_sb[:].unsqueeze(1).unsqueeze(3).to_broadcast([P, n // 2, 4, 2]),
+                    op=MULT,
+                )
+            elif op[0] == "W":
+                x = int(op[1]) % W_BUFS
+                lo, n = span(op[1:])
+                quantize(
+                    w_codes[x][:, lo : lo + n],
+                    w_scales[x][:, lo : lo + n],
+                    w_bf[x][:, lo : lo + n, :].rearrange("p n r -> p (n r)"),
+                )
+            elif op[0] == "P":
+                h = int(op[1])
+                lo, n = span(op[1:])
+                y_ps = y_banks[len(y_of) % Y_BANKS]
+                y_of[op[1:]] = y_ps
+                for b in range(n // 128):
+                    qc = slice(lo + 128 * b, lo + 128 * (b + 1))
+                    vc = slice(128 * h, 128 * (h + 1))
+                    nc.tensor.matmul_mx(
+                        out=y_ps[:, qc],
+                        lhsT=w_codes[h % W_BUFS][:, qc].bitcast(FP8X4),
+                        lhsT_scale=w_scales[h % W_BUFS][:, qc],
+                        rhs=v_codes[:, vc].bitcast(FP8X4),
+                        rhs_scale=v_scales[:, vc],
+                        start=True,
+                        stop=True,
+                    )
+            elif op[0] == "G":
+                h = int(op[1])
+                nc.scalar.activation(out=raw["g", h], in_=raw["g", h], func=SIGMOID)
+            else:
+                h = int(op[1])
+                lo, n = span(op[1:])
+                res = raw["g", h][:, lo : lo + n]
+                nc.vector.scalar_tensor_tensor(
+                    out=res,
+                    in0=y_of[op[1:]][:, lo : lo + n],
+                    scalar=1.0 / 16.0,
+                    in1=res,
+                    op0=MULT,
+                    op1=MULT,
+                )
+                dst = out[h].rearrange("(u m c) e -> m u (c e)", u=2, c=2)
+                if n == 512:
+                    nc.sync.dma_start(out=dst, in_=res.rearrange("p (u x) -> p u x", u=2))
+                else:
+                    nc.sync.dma_start(out=dst[:, lo // 256, :], in_=res)

@@ -11,27 +11,40 @@ U32 = mybir.dt.uint32
 U8 = mybir.dt.uint8
 FP8X4 = mybir.dt.float8_e4m3fn_x4
 SIGMOID = mybir.ActivationFunctionType.Sigmoid
+COPY = mybir.ActivationFunctionType.Copy
 MULT = mybir.AluOpType.mult
 
 P = 128
-ROWS = 32
-BANKS = (2, 1, 1, 2)
-Y_BANKS = 2
-P_BUFS = 8
-W_BUFS = 8
+PACK = 4
+ROWS = D // PACK
+SET = P // ROWS
+BLOCK = 128
+HALF = NQ // 2
+SPANS = {"": (0, NQ), "a": (0, HALF), "b": (HALF, HALF), "w": (0, BLOCK), "x": (BLOCK, BLOCK)}
 
-LOADS = "Lk0a Lk0b Lq0a Lq0b Lk1 Lq1 Lv45 Lv23 Lv67 Lg45 Lg01 Lg67 Lv01 Lg23".split()
-ORDER = """
-S:ck0a ck0b qk023 qk01 qk00 cq0a qq0a cq0b M0a0 M0a1 qq0b A0a1 A0a0 M10 A0a2 A0a3
-M30 A10 ck1a1 M31 ck1a0 A30 T0a M12 A31 M33 A12 ck1b0 M32 ck1b1 A33 M0b0
-cq1a0 cq1b0 A32 M11 cq1b1 cq1a1 A0b1 M0b1 qk1 A11 M20 qq1 A0b2 M13 A0b0 T3
-A0b3 M7a0 A20 M41 A13 M21 A7a0 A41 M42 T0b A21 M52 A42 T1 M22 A52
-M43 A22 M40 A43 M23 W0 A40 M50 W1 A23 M7a1 T4 S:cv1 A50 S:cv5 M51
-S:cv0 M62 T2 S:cv4 A7a1 A7a2 A51 A62 M53 qv01 W4 G0 M61 qv45 A53 M7b0
-W3 A61 P4 T5 S:cv2 P0 G4 M60 A7a3 A7b1 M7b1 A60 W2 S:cv7 F4 M63
-T7a A7b3 A7b0 G6 F0 A63 W7a S:cv3 W5 G2 T6 P5 G5 P1 G7 S:cv6
-G1 F5 A7b2 qv23 G3 qv67 F1 P3 W6 P7a F3 F7a P6 T7b P2 F6
-W7b F2 P7b F7b
+SCORE_BANKS = (2, 1, 1, 2)
+Y_BANKS = 2
+
+LOADS = "k0 q0a q0b k1 v01 v23 q1 v45 g01 g23 v67 g45 g67".split()
+
+STEPS = """
+cast_k:0.23@S cast_k:0.01 quant_k:0.01 cast_q:0x@S cast_q:0w quant_q:0w quant_k:0.23 scores:0w.01 quant_q:0x
+cast_q:0b scores:0w.23 sigmoid:0w.0 sigmoid:0w.1 sigmoid:0w.2 quant_q:0b scores:0x.01 sigmoid:0w.3
+scores:0x.23 weigh:0w sigmoid:0x.0 scores:1.0 sigmoid:0x.1 sigmoid:0x.2 sigmoid:0x.3 cast_k:1.0123
+scores:2.0 sigmoid:1.0 scores:0b.01 sigmoid:2.0 cast_v:0 scores:0b.23 cast_v:1 sigmoid:0b.0 quant_k:1.0123
+sigmoid:0b.1 scores:1.1 sigmoid:0b.2 quant_v:01 sigmoid:0b.3 scores:2.1 weigh:0x sigmoid:1.1 scores:3.0
+cast_v:2 cast_v:3@S weigh:0b scores:1.2 sigmoid:2.1 scores:3.1 sigmoid:3.0 quant_v:23 cast_q:1a sigmoid:1.2
+scores:2.2 cast_q:1b sigmoid:3.1 scores:1.3 sigmoid:2.2 quant_w:0 scores:3.2 sigmoid:1.3 quant_q:1
+scores:2.3 cast_v:5@S cast_v:4 scores:3.3 weigh:1 sigmoid:3.2 scores:4.0 sigmoid:2.3 scores:5.0 gate:0
+sigmoid:3.3 scores:6.0 weigh:2 gate:1 scores:4.1 sigmoid:4.0 mix:0 sigmoid:5.0 sigmoid:6.0 scores:5.1
+weigh:3 sigmoid:4.1 scores:6.1 cast_v:6@S scores:4.2 sigmoid:5.1 scores:4.3 sigmoid:6.1 quant_w:1 scores:5.2
+cast_v:7@S quant_w:2 scores:7a.01 sigmoid:4.2 quant_v:45 finish:0 sigmoid:4.3 scores:6.2 quant_w:3
+sigmoid:5.2 mix:1 weigh:4 sigmoid:7a.0 scores:5.3 scale:6.0 gate:2 mix:2 sigmoid:7a.1 sigmoid:6.2 quant_v:67
+sigmoid:5.3 quant_w:4 scores:6.3 scale:6.1 finish:1 scores:7a.23 scale:6.2 weigh:5 scores:7b.01 sigmoid:6.3
+mix:3 gate:3 scale:6.3 sigmoid:7a.2 finish:2 scale:7a.0 sigmoid:7b.0 weave:6 mix:4 sigmoid:7a.3 scale:7a.1
+scores:7b.23 sigmoid:7b.1 scale:7a.2 quant_w:5 scale:7a.3 scale:7b.0 quant_w:6 gate:4 finish:3 sigmoid:7b.2
+scale:7b.1 weave:7a mix:5 sigmoid:7b.3 scale:7b.2 finish:4 scale:7b.3 gate:5 quant_w:7a mix:6 weave:7b
+gate:6 finish:5 gate:7 quant_w:7b mix:7a finish:6 finish:7a mix:7b finish:7b
 """.split()
 
 
@@ -42,194 +55,172 @@ def tile_rows_a_sigmoid_kb_gate_kernel(tc, qT, kT, t, v, kb, og, out):
         ps = ctx.enter_context(tc.psum_pool(name="ps", bufs=1))
         ctx.enter_context(tc.manual_schedule())
 
-        def tiles(name, count, shape, dtype, pool=sb):
-            if pool is ps:
-                return [pool.tile(shape, dtype, name="%s%d" % (name, i)) for i in range(count)]
-            return [pool.tile(shape, dtype, name="%s%d" % (name, i), align_bytes=64) for i in range(count)]
+        def tile(name, shape, dtype):
+            return sb.tile(shape, dtype, name=name, align_bytes=64)
 
-        t_sb, kb_sb = tiles("col", 2, [P, 4], F32)
-        nc.scalar.dma_start(out=kb_sb[:], in_=kb.rearrange("(p j) o -> p (j o)", j=4))
-        nc.scalar.dma_start(out=t_sb[:], in_=t.rearrange("(p j) o -> p (j o)", j=4))
+        def mx_tiles(name, columns):
+            return (
+                tile(name + "_bf", [P, columns * PACK], BF16),
+                tile(name + "_codes", [P, columns], U32),
+                tile(name + "_scales", [P, columns], U8),
+            )
+
+        kb_sb = tile("kb", [P, PACK], F32)
+        t_sb = tile("t", [P, PACK], F32)
+        nc.scalar.dma_start(out=kb_sb[:], in_=kb.rearrange("(p r) o -> p (r o)", r=PACK))
+        nc.scalar.dma_start(out=t_sb[:], in_=t.rearrange("(p r) o -> p (r o)", r=PACK))
+
+        warm = tile("warm", [P, 2], F32)
+        nc.gpsimd.memset(warm[:, 0:1], 0.0)
+        nc.scalar.activation(out=warm[:, 1:2], in_=warm[:, 0:1], func=SIGMOID)
 
         raw = {}
         for name in LOADS:
-            kind = name[1]
+            kind, first = name[0], int(name[1])
             if kind in "qk":
-                s = int(name[2])
-                src = (qT if kind == "q" else kT)[4 * s : 4 * s + 4].rearrange("g (p j) n -> (g p) j n", j=4)
-                if len(name) == 4:
-                    u = "ab".index(name[3])
-                    tl = sb.tile([P, 4, 256], F32, name=name, align_bytes=64)
-                    nc.sync.dma_start(out=tl[:], in_=src[:, :, 256 * u : 256 * u + 256])
-                    raw[kind, s, u] = tl[:]
+                heads = (qT if kind == "q" else kT)[SET * first : SET * (first + 1)]
+                src = heads.rearrange("g (p j) n -> (g p) j n", j=PACK)
+                lo, width = SPANS[name[2:]]
+                dst = tile("raw_" + name, [P, PACK, width], F32)
+                nc.sync.dma_start(out=dst[:], in_=src[:, :, lo : lo + width])
+                if kind == "k":
+                    raw["k", first] = dst[:]
                 else:
-                    tl = sb.tile([P, 4, 512], F32, name=name, align_bytes=64)
-                    nc.sync.dma_start(out=tl[:], in_=src)
-                    for u in range(2):
-                        raw[kind, s, u] = tl[:, :, 256 * u : 256 * u + 256]
+                    for x in range(0, width, HALF):
+                        raw["q", first, (lo + x) // HALF] = dst[:, :, x : x + HALF]
             else:
-                h0, cnt = int(name[2]), len(name) - 2
-                tl = sb.tile([P, cnt, 512], F32, name=name, align_bytes=64)
+                dst = tile("raw_" + name, [P, 2, PACK * E], F32)
                 if kind == "v":
-                    nc.sync.dma_start(out=tl[:], in_=v[h0 : h0 + cnt].rearrange("h (p j) e -> p h (j e)", j=4))
+                    nc.sync.dma_start(
+                        out=dst[:], in_=v[first : first + 2].rearrange("h (p r) e -> p h (r e)", r=PACK)
+                    )
                 else:
                     nc.sync.dma_start(
-                        out=tl[:].rearrange("p h (u x) -> p (h u) x", u=2),
-                        in_=og[h0 : h0 + cnt].rearrange("h (u m c) e -> m (h u) (c e)", u=2, c=2),
+                        out=dst[:].rearrange("p h (u x) -> p (h u) x", u=2),
+                        in_=og[first : first + 2].rearrange("h (u m c) e -> m (h u) (c e)", u=2, c=2),
                     )
-                for i in range(cnt):
-                    raw[kind, h0 + i] = tl[:, i, :]
+                raw[kind, first], raw[kind, first + 1] = dst[:, 0, :], dst[:, 1, :]
 
-        q_bf = tiles("q_bf", 2, [P, 2, 2, 128, 4], BF16)
-        k_bf = tiles("k_bf", 2, [P, 4, 128, 4], BF16)
-        v_bf = tiles("v_bf", 1, [P, H, 128, 4], BF16)[0]
-        q_codes = tiles("q_codes", 2, [P, 512], U32)
-        k_codes = tiles("k_codes", 2, [P, 512], U32)
-        v_codes = tiles("v_codes", 1, [P, H * 128], U32)[0]
-        q_scales = tiles("q_scales", 2, [P, 512], U8)
-        k_scales = tiles("k_scales", 2, [P, 512], U8)
-        v_scales = tiles("v_scales", 1, [P, H * 128], U8)[0]
-        p_sb = tiles("p", P_BUFS, [P, 4, 512], F32)
-        w_bf = tiles("w_bf", W_BUFS, [P, 512, 4], BF16)
-        w_codes = tiles("w_codes", W_BUFS, [P, 512], U32)
-        w_scales = tiles("w_scales", W_BUFS, [P, 512], U8)
-        banks = [tiles("score%d_" % g, BANKS[g], [P, 512], F32, ps) for g in range(4)]
-        y_banks = tiles("y", Y_BANKS, [P, 512], F32, ps)
-        y_of = {}
-        used = [0, 0, 0, 0]
-        where = {}
+        q_mx = [mx_tiles("q%d" % s, NQ) for s in range(H // SET)]
+        k_mx = [mx_tiles("k%d" % s, N) for s in range(H // SET)]
+        v_mx = mx_tiles("v", H * E)
+        w_mx = [mx_tiles("w%d" % h, NQ) for h in range(H)]
+        score_banks = [
+            [ps.tile([P, NQ], F32, name="score%d_%d" % (g, b)) for b in range(SCORE_BANKS[g])] for g in range(SET)
+        ]
+        y_banks = [ps.tile([P, NQ], F32, name="y%d" % b) for b in range(Y_BANKS)]
+        fills = [0] * SET
+        scores_of, p_of, pt_of, y_of = {}, {}, {}, {}
 
-        def copy(eng, dst, src):
-            if eng == "S":
+        def cast(on_scalar, dst, src):
+            if on_scalar:
                 nc.scalar.copy(out=dst, in_=src)
-            elif eng == "G":
-                nc.gpsimd.tensor_scalar(out=dst, in0=src, scalar1=1.0, scalar2=1.0, op0=MULT, op1=MULT)
             else:
                 nc.vector.tensor_copy(out=dst, in_=src)
 
-        def quantize(codes, scales, src):
-            nc.vector.quantize_mx(out=codes.bitcast(FP8X4), scales=scales, in_=src)
+        def quantize(mx, lo, width):
+            values, codes, scales = mx
+            nc.vector.quantize_mx(
+                out=codes[:, lo : lo + width].bitcast(FP8X4),
+                scales=scales[:, lo : lo + width],
+                in_=values[:, PACK * lo : PACK * (lo + width)],
+            )
 
-        def span(unit):
-            return (0, 512) if len(unit) == 1 else (256 * "ab".index(unit[1]), 256)
+        def matmul(dst, rows, left, left_lo, right, right_lo):
+            left_cols, right_cols = slice(left_lo, left_lo + BLOCK), slice(right_lo, right_lo + BLOCK)
+            nc.tensor.matmul_mx(
+                out=dst,
+                lhsT=left[1][rows, left_cols].bitcast(FP8X4),
+                lhsT_scale=left[2][rows, left_cols],
+                rhs=right[1][rows, right_cols].bitcast(FP8X4),
+                rhs_scale=right[2][rows, right_cols],
+                start=True,
+                stop=True,
+            )
 
-        for item in ORDER:
-            eng, op = item.split(":") if ":" in item else ("V", item)
-            if op[:2] in ("cq", "ck"):
-                s, u = int(op[2]), "ab".index(op[3])
-                lo, n = (0, 256) if len(op) == 4 else (128 * int(op[4]), 128)
-                src = raw[op[1], s, u][:, :, lo : lo + n]
-                if op[1] == "q":
-                    dst = q_bf[s][:, u, :, lo // 2 : (lo + n) // 2, :]
-                    copy(eng, dst.rearrange("p c m j -> p m j c"), src.rearrange("p j (m c) -> p m j c", c=2))
-                else:
-                    s0 = (256 * u + lo) // 4
-                    dst = k_bf[s][:, :, s0 : s0 + n // 4, :]
-                    copy(eng, dst.rearrange("p r s j -> p s j r"), src.rearrange("p j (s r) -> p s j r", r=4))
-            elif op[:2] == "cv":
-                h = int(op[2])
-                copy(
-                    eng,
-                    v_bf[:, h, :, :].rearrange("p (c i) j -> p c j i", i=2),
-                    raw["v", h].rearrange("p (j c i) -> p c j i", j=4, i=2),
-                )
-            elif op[:2] == "qq":
-                s = int(op[2])
-                lo, n = span(op[2:])
-                flat = q_bf[s][:].rearrange("p u c m j -> p (u c m j)")
-                quantize(q_codes[s][:, lo : lo + n], q_scales[s][:, lo : lo + n], flat[:, 4 * lo : 4 * (lo + n)])
-            elif op[:2] == "qk":
-                s = int(op[2])
-                lo, n = (0, 512) if len(op) == 3 else (128 * int(op[3]), 128 * (len(op) - 3))
-                flat = k_bf[s][:].rearrange("p r s j -> p (r s j)")
-                quantize(k_codes[s][:, lo : lo + n], k_scales[s][:, lo : lo + n], flat[:, 4 * lo : 4 * (lo + n)])
-            elif op[:2] == "qv":
-                lo, n = 128 * int(op[2]), 128 * (len(op) - 2)
-                flat = v_bf[:].rearrange("p h e j -> p (h e j)")
-                quantize(v_codes[:, lo : lo + n], v_scales[:, lo : lo + n], flat[:, 4 * lo : 4 * (lo + n)])
-            elif op[0] == "M":
-                unit, i = op[1:-1], int(op[-1])
-                h = int(unit[0])
-                s, g = divmod(h, 4)
-                lo, n = span(unit)
-                bank = banks[g][used[g] % BANKS[g]]
-                used[g] += 1
-                rows = slice(ROWS * g, ROWS * (g + 1))
-                rs = [i] if n == 512 else [2 * i, 2 * i + 1]
-                for x, r in enumerate(rs):
-                    where[unit, r] = bank[:, x * n : (x + 1) * n]
-                    for b in range(n // 128):
-                        qc = slice(lo + 128 * b, lo + 128 * (b + 1))
-                        kc = slice(128 * r, 128 * (r + 1))
-                        nc.tensor.matmul_mx(
-                            out=bank[:, x * n + 128 * b : x * n + 128 * (b + 1)],
-                            lhsT=k_codes[s][rows, kc].bitcast(FP8X4),
-                            lhsT_scale=k_scales[s][rows, kc],
-                            rhs=q_codes[s][rows, qc].bitcast(FP8X4),
-                            rhs_scale=q_scales[s][rows, qc],
-                            start=True,
-                            stop=True,
-                        )
-            elif op[0] == "A":
-                unit, r = op[1:-1], int(op[-1])
-                lo, n = span(unit)
-                nc.scalar.activation(
-                    out=p_sb[int(unit[0]) % P_BUFS][:, r, lo : lo + n],
-                    in_=where[unit, r],
-                    func=SIGMOID,
-                    bias=kb_sb[:, r : r + 1],
-                )
-            elif op[0] == "T":
-                h = int(op[1])
-                lo, n = span(op[1:])
-                nc.vector.tensor_tensor(
-                    out=w_bf[h % W_BUFS][:, lo : lo + n, :].rearrange("p (c i) r -> p c r i", i=2),
-                    in0=p_sb[h % P_BUFS][:, :, lo : lo + n].rearrange("p r (c i) -> p c r i", i=2),
-                    in1=t_sb[:].unsqueeze(1).unsqueeze(3).to_broadcast([P, n // 2, 4, 2]),
-                    op=MULT,
-                )
-            elif op[0] == "W":
-                x = int(op[1]) % W_BUFS
-                lo, n = span(op[1:])
-                quantize(
-                    w_codes[x][:, lo : lo + n],
-                    w_scales[x][:, lo : lo + n],
-                    w_bf[x][:, lo : lo + n, :].rearrange("p n r -> p (n r)"),
-                )
-            elif op[0] == "P":
-                h = int(op[1])
-                lo, n = span(op[1:])
-                y_ps = y_banks[len(y_of) % Y_BANKS]
-                y_of[op[1:]] = y_ps
-                for b in range(n // 128):
-                    qc = slice(lo + 128 * b, lo + 128 * (b + 1))
-                    vc = slice(128 * h, 128 * (h + 1))
-                    nc.tensor.matmul_mx(
-                        out=y_ps[:, qc],
-                        lhsT=w_codes[h % W_BUFS][:, qc].bitcast(FP8X4),
-                        lhsT_scale=w_scales[h % W_BUFS][:, qc],
-                        rhs=v_codes[:, vc].bitcast(FP8X4),
-                        rhs_scale=v_scales[:, vc],
-                        start=True,
-                        stop=True,
-                    )
-            elif op[0] == "G":
-                h = int(op[1])
-                nc.scalar.activation(out=raw["g", h], in_=raw["g", h], func=SIGMOID)
+        def column_pairs(values, lo, width):
+            words = values[:, PACK * lo : PACK * (lo + width)]
+            return words.rearrange("p (c i r) -> p c r i", i=2, r=PACK)
+
+        def row_pairs(rows):
+            return rows.rearrange("p r (c i) -> p c r i", i=2)
+
+        for step in STEPS:
+            verb, arg = step.replace("@S", "").split(":")
+            on_scalar = "@S" in step
+            unit = arg.split(".")[0]
+            tiles = [int(r) for r in arg.split(".")[1]] if "." in arg else []
+            index = int(unit[0])
+            if verb == "cast_k":
+                r = slice(tiles[0], tiles[-1] + 1)
+                dst = k_mx[index][0][:].rearrange("p (r m j) -> p r m j", r=PACK, j=PACK)[:, r, :, :]
+                src = raw["k", index].rearrange("p j (m r) -> p m j r", r=PACK)[:, :, :, r]
+                cast(on_scalar, dst.rearrange("p r m j -> p m j r"), src)
+            elif verb == "quant_k":
+                quantize(k_mx[index], BLOCK * tiles[0], BLOCK * len(tiles))
+            elif verb == "cast_v":
+                src = raw["v", index].rearrange("p (r e) -> p r e", r=PACK)
+                cast(on_scalar, column_pairs(v_mx[0], E * index, E), row_pairs(src))
+            elif verb == "quant_v":
+                quantize(v_mx, E * index, E * len(unit))
+            elif verb == "gate":
+                nc.scalar.activation(out=raw["g", index], in_=raw["g", index], func=SIGMOID)
             else:
-                h = int(op[1])
-                lo, n = span(op[1:])
-                res = raw["g", h][:, lo : lo + n]
-                nc.vector.scalar_tensor_tensor(
-                    out=res,
-                    in0=y_of[op[1:]][:, lo : lo + n],
-                    scalar=1.0 / 16.0,
-                    in1=res,
-                    op0=MULT,
-                    op1=MULT,
-                )
-                dst = out[h].rearrange("(u m c) e -> m u (c e)", u=2, c=2)
-                if n == 512:
-                    nc.sync.dma_start(out=dst, in_=res.rearrange("p (u x) -> p u x", u=2))
+                lo, width = SPANS[unit[1:]]
+                s, g = divmod(index, SET)
+                if verb == "cast_q" and width == BLOCK:
+                    src = raw["q", index, lo // HALF].rearrange("p j (m c) -> p j m c", c=2)[:, :, :, lo // BLOCK % 2]
+                    cast(on_scalar, column_pairs(q_mx[index][0], lo, width), row_pairs(src))
+                elif verb == "cast_q":
+                    dst = q_mx[index][0][:, PACK * lo : PACK * (lo + width)]
+                    src = raw["q", index, lo // HALF].rearrange("p j (m c) -> p m j c", c=2)
+                    cast(on_scalar, dst.rearrange("p (c m j) -> p m j c", c=2, j=PACK), src)
+                elif verb == "quant_q":
+                    quantize(q_mx[index], lo, width)
+                elif verb == "scores":
+                    bank = score_banks[g][fills[g] % SCORE_BANKS[g]]
+                    fills[g] += 1
+                    rows = slice(ROWS * g, ROWS * (g + 1))
+                    for place, r in enumerate(tiles):
+                        scores_of[unit, r] = bank[:, place * width : (place + 1) * width]
+                        for x in range(0, width, BLOCK):
+                            matmul(scores_of[unit, r][:, x : x + BLOCK], rows, k_mx[s], BLOCK * r, q_mx[s], lo + x)
+                elif verb == "sigmoid":
+                    r = tiles[0]
+                    if unit not in p_of:
+                        p_of[unit] = tile("p" + unit, [P, PACK, width], F32)
+                    nc.scalar.activation(
+                        out=p_of[unit][:, r, :], in_=scores_of[unit, r], func=SIGMOID, bias=kb_sb[:, r : r + 1]
+                    )
+                elif verb == "weigh":
+                    nc.vector.tensor_tensor(
+                        out=column_pairs(w_mx[index][0], lo, width),
+                        in0=row_pairs(p_of[unit][:]),
+                        in1=t_sb[:].unsqueeze(1).unsqueeze(3).to_broadcast([P, width // 2, PACK, 2]),
+                        op=MULT,
+                    )
+                elif verb == "scale":
+                    r = tiles[0]
+                    if unit not in pt_of:
+                        pt_of[unit] = tile("pt" + unit, [P, PACK, width], BF16)
+                    nc.scalar.activation(
+                        out=pt_of[unit][:, r, :], in_=p_of[unit][:, r, :], func=COPY, scale=t_sb[:, r : r + 1]
+                    )
+                elif verb == "weave":
+                    nc.vector.tensor_copy(out=column_pairs(w_mx[index][0], lo, width), in_=row_pairs(pt_of[unit][:]))
+                elif verb == "quant_w":
+                    quantize(w_mx[index], lo, width)
+                elif verb == "mix":
+                    y_of[unit] = y_banks[len(y_of) % Y_BANKS][:, lo : lo + width]
+                    for x in range(0, width, BLOCK):
+                        matmul(y_of[unit][:, x : x + BLOCK], slice(0, P), w_mx[index], lo + x, v_mx, E * index)
                 else:
-                    nc.sync.dma_start(out=dst[:, lo // 256, :], in_=res)
+                    gated = raw["g", index][:, lo : lo + width]
+                    nc.vector.scalar_tensor_tensor(
+                        out=gated, in0=y_of[unit], scalar=1.0 / 16.0, in1=gated, op0=MULT, op1=MULT
+                    )
+                    rows_out = out[index].rearrange("(u m c) e -> m u (c e)", u=2, c=2)
+                    nc.sync.dma_start(
+                        out=rows_out[:, lo // HALF : (lo + width) // HALF, :],
+                        in_=gated.rearrange("p (u x) -> p u x", x=HALF),
+                    )

from contextlib import ExitStack

import concourse.mybir as mybir

H, D, NQ, N, E = 8, 128, 512, 512, 128
FLOPS = 2 * H * N * NQ * (D + E)

F32 = mybir.dt.float32
BF16 = mybir.dt.bfloat16
U32 = mybir.dt.uint32
U8 = mybir.dt.uint8
FP8X4 = mybir.dt.float8_e4m3fn_x4
SIGMOID = mybir.ActivationFunctionType.Sigmoid
COPY = mybir.ActivationFunctionType.Copy
MULT = mybir.AluOpType.mult

P = 128
PACK = 4
ROWS = D // PACK
SET = P // ROWS
BLOCK = 128
HALF = NQ // 2
SPANS = {"": (0, NQ), "a": (0, HALF), "b": (HALF, HALF), "w": (0, BLOCK), "x": (BLOCK, BLOCK)}

SCORE_BANKS = (2, 1, 1, 2)
Y_BANKS = 2

LOADS = "k0 q0a q0b k1 v01 v23 q1 v45 g01 g23 v67 g45 g67".split()

STEPS = """
cast_k:0.23@S cast_k:0.01 quant_k:0.01 cast_q:0x@S cast_q:0w quant_q:0w quant_k:0.23 scores:0w.01 quant_q:0x
cast_q:0b scores:0w.23 sigmoid:0w.0 sigmoid:0w.1 sigmoid:0w.2 quant_q:0b scores:0x.01 sigmoid:0w.3
scores:0x.23 weigh:0w sigmoid:0x.0 scores:1.0 sigmoid:0x.1 sigmoid:0x.2 sigmoid:0x.3 cast_k:1.0123
scores:2.0 sigmoid:1.0 scores:0b.01 sigmoid:2.0 cast_v:0 scores:0b.23 cast_v:1 sigmoid:0b.0 quant_k:1.0123
sigmoid:0b.1 scores:1.1 sigmoid:0b.2 quant_v:01 sigmoid:0b.3 scores:2.1 weigh:0x sigmoid:1.1 scores:3.0
cast_v:2 cast_v:3@S weigh:0b scores:1.2 sigmoid:2.1 scores:3.1 sigmoid:3.0 quant_v:23 cast_q:1a sigmoid:1.2
scores:2.2 cast_q:1b sigmoid:3.1 scores:1.3 sigmoid:2.2 quant_w:0 scores:3.2 sigmoid:1.3 quant_q:1
scores:2.3 cast_v:5@S cast_v:4 scores:3.3 weigh:1 sigmoid:3.2 scores:4.0 sigmoid:2.3 scores:5.0 gate:0
sigmoid:3.3 scores:6.0 weigh:2 gate:1 scores:4.1 sigmoid:4.0 mix:0 sigmoid:5.0 sigmoid:6.0 scores:5.1
weigh:3 sigmoid:4.1 scores:6.1 cast_v:6@S scores:4.2 sigmoid:5.1 scores:4.3 sigmoid:6.1 quant_w:1 scores:5.2
cast_v:7@S quant_w:2 scores:7a.01 sigmoid:4.2 quant_v:45 finish:0 sigmoid:4.3 scores:6.2 quant_w:3
sigmoid:5.2 mix:1 weigh:4 sigmoid:7a.0 scores:5.3 scale:6.0 gate:2 mix:2 sigmoid:7a.1 sigmoid:6.2 quant_v:67
sigmoid:5.3 quant_w:4 scores:6.3 scale:6.1 finish:1 scores:7a.23 scale:6.2 weigh:5 scores:7b.01 sigmoid:6.3
mix:3 gate:3 scale:6.3 sigmoid:7a.2 finish:2 scale:7a.0 sigmoid:7b.0 weave:6 mix:4 sigmoid:7a.3 scale:7a.1
scores:7b.23 sigmoid:7b.1 scale:7a.2 quant_w:5 scale:7a.3 scale:7b.0 quant_w:6 gate:4 finish:3 sigmoid:7b.2
scale:7b.1 weave:7a mix:5 sigmoid:7b.3 scale:7b.2 finish:4 scale:7b.3 gate:5 quant_w:7a mix:6 weave:7b
gate:6 finish:5 gate:7 quant_w:7b mix:7a finish:6 finish:7a mix:7b finish:7b
""".split()


def tile_rows_a_sigmoid_kb_gate_kernel(tc, qT, kT, t, v, kb, og, out):
    nc = tc.nc
    with ExitStack() as ctx:
        sb = ctx.enter_context(tc.tile_pool(name="sb", bufs=1))
        ps = ctx.enter_context(tc.psum_pool(name="ps", bufs=1))
        ctx.enter_context(tc.manual_schedule())

        def tile(name, shape, dtype):
            return sb.tile(shape, dtype, name=name, align_bytes=64)

        def mx_tiles(name, columns):
            return (
                tile(name + "_bf", [P, columns * PACK], BF16),
                tile(name + "_codes", [P, columns], U32),
                tile(name + "_scales", [P, columns], U8),
            )

        kb_sb = tile("kb", [P, PACK], F32)
        t_sb = tile("t", [P, PACK], F32)
        nc.scalar.dma_start(out=kb_sb[:], in_=kb.rearrange("(p r) o -> p (r o)", r=PACK))
        nc.scalar.dma_start(out=t_sb[:], in_=t.rearrange("(p r) o -> p (r o)", r=PACK))

        warm = tile("warm", [P, 2], F32)
        nc.gpsimd.memset(warm[:, 0:1], 0.0)
        nc.scalar.activation(out=warm[:, 1:2], in_=warm[:, 0:1], func=SIGMOID)

        raw = {}
        for name in LOADS:
            kind, first = name[0], int(name[1])
            if kind in "qk":
                heads = (qT if kind == "q" else kT)[SET * first : SET * (first + 1)]
                src = heads.rearrange("g (p j) n -> (g p) j n", j=PACK)
                lo, width = SPANS[name[2:]]
                dst = tile("raw_" + name, [P, PACK, width], F32)
                nc.sync.dma_start(out=dst[:], in_=src[:, :, lo : lo + width])
                if kind == "k":
                    raw["k", first] = dst[:]
                else:
                    for x in range(0, width, HALF):
                        raw["q", first, (lo + x) // HALF] = dst[:, :, x : x + HALF]
            else:
                dst = tile("raw_" + name, [P, 2, PACK * E], F32)
                if kind == "v":
                    nc.sync.dma_start(
                        out=dst[:], in_=v[first : first + 2].rearrange("h (p r) e -> p h (r e)", r=PACK)
                    )
                else:
                    nc.sync.dma_start(
                        out=dst[:].rearrange("p h (u x) -> p (h u) x", u=2),
                        in_=og[first : first + 2].rearrange("h (u m c) e -> m (h u) (c e)", u=2, c=2),
                    )
                raw[kind, first], raw[kind, first + 1] = dst[:, 0, :], dst[:, 1, :]

        q_mx = [mx_tiles("q%d" % s, NQ) for s in range(H // SET)]
        k_mx = [mx_tiles("k%d" % s, N) for s in range(H // SET)]
        v_mx = mx_tiles("v", H * E)
        w_mx = [mx_tiles("w%d" % h, NQ) for h in range(H)]
        score_banks = [
            [ps.tile([P, NQ], F32, name="score%d_%d" % (g, b)) for b in range(SCORE_BANKS[g])] for g in range(SET)
        ]
        y_banks = [ps.tile([P, NQ], F32, name="y%d" % b) for b in range(Y_BANKS)]
        fills = [0] * SET
        scores_of, p_of, pt_of, y_of = {}, {}, {}, {}

        def cast(on_scalar, dst, src):
            if on_scalar:
                nc.scalar.copy(out=dst, in_=src)
            else:
                nc.vector.tensor_copy(out=dst, in_=src)

        def quantize(mx, lo, width):
            values, codes, scales = mx
            nc.vector.quantize_mx(
                out=codes[:, lo : lo + width].bitcast(FP8X4),
                scales=scales[:, lo : lo + width],
                in_=values[:, PACK * lo : PACK * (lo + width)],
            )

        def matmul(dst, rows, left, left_lo, right, right_lo):
            left_cols, right_cols = slice(left_lo, left_lo + BLOCK), slice(right_lo, right_lo + BLOCK)
            nc.tensor.matmul_mx(
                out=dst,
                lhsT=left[1][rows, left_cols].bitcast(FP8X4),
                lhsT_scale=left[2][rows, left_cols],
                rhs=right[1][rows, right_cols].bitcast(FP8X4),
                rhs_scale=right[2][rows, right_cols],
                start=True,
                stop=True,
            )

        def column_pairs(values, lo, width):
            words = values[:, PACK * lo : PACK * (lo + width)]
            return words.rearrange("p (c i r) -> p c r i", i=2, r=PACK)

        def row_pairs(rows):
            return rows.rearrange("p r (c i) -> p c r i", i=2)

        for step in STEPS:
            verb, arg = step.replace("@S", "").split(":")
            on_scalar = "@S" in step
            unit = arg.split(".")[0]
            tiles = [int(r) for r in arg.split(".")[1]] if "." in arg else []
            index = int(unit[0])
            if verb == "cast_k":
                r = slice(tiles[0], tiles[-1] + 1)
                dst = k_mx[index][0][:].rearrange("p (r m j) -> p r m j", r=PACK, j=PACK)[:, r, :, :]
                src = raw["k", index].rearrange("p j (m r) -> p m j r", r=PACK)[:, :, :, r]
                cast(on_scalar, dst.rearrange("p r m j -> p m j r"), src)
            elif verb == "quant_k":
                quantize(k_mx[index], BLOCK * tiles[0], BLOCK * len(tiles))
            elif verb == "cast_v":
                src = raw["v", index].rearrange("p (r e) -> p r e", r=PACK)
                cast(on_scalar, column_pairs(v_mx[0], E * index, E), row_pairs(src))
            elif verb == "quant_v":
                quantize(v_mx, E * index, E * len(unit))
            elif verb == "gate":
                nc.scalar.activation(out=raw["g", index], in_=raw["g", index], func=SIGMOID)
            else:
                lo, width = SPANS[unit[1:]]
                s, g = divmod(index, SET)
                if verb == "cast_q" and width == BLOCK:
                    src = raw["q", index, lo // HALF].rearrange("p j (m c) -> p j m c", c=2)[:, :, :, lo // BLOCK % 2]
                    cast(on_scalar, column_pairs(q_mx[index][0], lo, width), row_pairs(src))
                elif verb == "cast_q":
                    dst = q_mx[index][0][:, PACK * lo : PACK * (lo + width)]
                    src = raw["q", index, lo // HALF].rearrange("p j (m c) -> p m j c", c=2)
                    cast(on_scalar, dst.rearrange("p (c m j) -> p m j c", c=2, j=PACK), src)
                elif verb == "quant_q":
                    quantize(q_mx[index], lo, width)
                elif verb == "scores":
                    bank = score_banks[g][fills[g] % SCORE_BANKS[g]]
                    fills[g] += 1
                    rows = slice(ROWS * g, ROWS * (g + 1))
                    for place, r in enumerate(tiles):
                        scores_of[unit, r] = bank[:, place * width : (place + 1) * width]
                        for x in range(0, width, BLOCK):
                            matmul(scores_of[unit, r][:, x : x + BLOCK], rows, k_mx[s], BLOCK * r, q_mx[s], lo + x)
                elif verb == "sigmoid":
                    r = tiles[0]
                    if unit not in p_of:
                        p_of[unit] = tile("p" + unit, [P, PACK, width], F32)
                    nc.scalar.activation(
                        out=p_of[unit][:, r, :], in_=scores_of[unit, r], func=SIGMOID, bias=kb_sb[:, r : r + 1]
                    )
                elif verb == "weigh":
                    nc.vector.tensor_tensor(
                        out=column_pairs(w_mx[index][0], lo, width),
                        in0=row_pairs(p_of[unit][:]),
                        in1=t_sb[:].unsqueeze(1).unsqueeze(3).to_broadcast([P, width // 2, PACK, 2]),
                        op=MULT,
                    )
                elif verb == "scale":
                    r = tiles[0]
                    if unit not in pt_of:
                        pt_of[unit] = tile("pt" + unit, [P, PACK, width], BF16)
                    nc.scalar.activation(
                        out=pt_of[unit][:, r, :], in_=p_of[unit][:, r, :], func=COPY, scale=t_sb[:, r : r + 1]
                    )
                elif verb == "weave":
                    nc.vector.tensor_copy(out=column_pairs(w_mx[index][0], lo, width), in_=row_pairs(pt_of[unit][:]))
                elif verb == "quant_w":
                    quantize(w_mx[index], lo, width)
                elif verb == "mix":
                    y_of[unit] = y_banks[len(y_of) % Y_BANKS][:, lo : lo + width]
                    for x in range(0, width, BLOCK):
                        matmul(y_of[unit][:, x : x + BLOCK], slice(0, P), w_mx[index], lo + x, v_mx, E * index)
                else:
                    gated = raw["g", index][:, lo : lo + width]
                    nc.vector.scalar_tensor_tensor(
                        out=gated, in0=y_of[unit], scalar=1.0 / 16.0, in1=gated, op0=MULT, op1=MULT
                    )
                    rows_out = out[index].rearrange("(u m c) e -> m u (c e)", u=2, c=2)
                    nc.sync.dma_start(
                        out=rows_out[:, lo // HALF : (lo + width) // HALF, :],
                        in_=gated.rearrange("p (u x) -> p u x", x=HALF),
                    )
